import numpy as np
import ml_dtypes


def mxq(x, axis, fmt="e4m3"):
    dtype, down = {"e4m3": (ml_dtypes.float8_e4m3fn, 7), "e5m2": (ml_dtypes.float8_e5m2, 14)}[fmt]
    v = np.moveaxis(np.asarray(x, np.float32).astype(ml_dtypes.bfloat16).astype(np.float64), axis, -1)
    blocks = v.reshape(v.shape[:-1] + (-1, 32))
    amax = np.abs(blocks).max(-1, keepdims=True)
    byte = np.maximum(np.where(amax > 0, np.frexp(amax)[1] - 1 + 127, 0) - down, 1)
    scale = np.exp2(byte - 127.0)
    codes = (blocks / scale).astype(np.float32).astype(dtype).astype(np.float64)
    return np.moveaxis((codes * scale).reshape(v.shape), -1, axis)


WIDE = False


def mx_kscale(k):
    if not WIDE:
        return np.ones(k)
    levels = np.array([10, -10, 5, -5, 0])
    if k % 512:
        return np.exp2(np.random.permutation(np.resize(levels, k // 32))).repeat(32)
    a = np.empty((k // 512, 16))
    for p in range(k // 512):
        a[p, :8] = np.random.permutation(np.resize(levels, 8))
        for g in range(8):
            far = levels[np.abs(levels - a[p, g]) >= 10]
            a[p, g + 8] = far[np.random.randint(len(far))]
    return np.exp2(a.ravel()).repeat(32)


def f64(x):
    return np.asarray(x).astype(np.float64)


def striped(idx):
    return np.tile(idx.reshape(-1, 16).T, (8, 1)).astype(np.uint16)


def unstriped(offs):
    return offs[:16].T.reshape(-1).astype(np.int64)


E2M1 = np.array([0.0, 0.5, 1.0, 1.5, 2.0, 3.0, 4.0, 6.0, -0.0, -0.5, -1.0, -1.5, -2.0, -3.0, -4.0, -6.0])


def pack_weight(w, fmt):
    k, n = w.shape
    w = f64(np.asarray(w, np.float32).astype(ml_dtypes.bfloat16)).reshape(k // 32, 32, n)
    amax = np.abs(w).max(1)
    if fmt == "e4m3":
        byte = np.frexp(amax)[1] - 1 + 127 - 7
    else:
        mant, ex = np.frexp(amax / 6.0)
        byte = np.where(mant > 0.5, ex, ex - 1) + 127
    byte = np.clip(np.where(amax > 0, byte, 1), 1, 254)
    scaled = (w * np.exp2(127.0 - byte)[:, None, :]).reshape(k, n).astype(np.float32)
    by_word = np.ascontiguousarray(scaled.reshape(k // 512, 128, 4, n).transpose(0, 1, 3, 2))
    if fmt == "e4m3":
        words = by_word.astype(ml_dtypes.float8_e4m3fn).view(np.uint8)
    else:
        c = by_word.astype(ml_dtypes.float4_e2m1fn).view(np.uint8) & 0xF
        words = (c[..., 0::2] | (c[..., 1::2] << 4)).reshape(k // 512, 128, 2 * n)
    return np.ascontiguousarray(words), np.ascontiguousarray(byte.astype(np.uint8).reshape(k // 512, 16, n))


def unpack_weight(words, scales, fmt):
    g, _, n = scales.shape
    words = np.ascontiguousarray(words).reshape(g, 128, n, -1)
    if fmt == "e4m3":
        vals = words.view(ml_dtypes.float8_e4m3fn).astype(np.float64)
    else:
        nib = np.empty((g, 128, n, 4), np.uint8)
        nib[..., 0::2] = words & 0xF
        nib[..., 1::2] = words >> 4
        vals = E2M1[nib]
    vals = vals * np.repeat(np.exp2(scales.astype(np.float64) - 127.0), 8, axis=1)[..., None]
    return vals.transpose(0, 1, 3, 2).reshape(g * 512, n)


def gelu(v):
    return 0.5 * v * (1.0 + np.tanh(np.sqrt(2.0 / np.pi) * (v + 0.044715 * v**3)))


K, T, S, H, T2, P, N = 1024, 2048, 512, 1024, 2048, 1024, 512

def setup_inputs():
    n = np.random.standard_normal
    s, u = mx_kscale(K)[:, None], mx_kscale(H)[:, None]
    perm = np.random.permutation(T2)
    d = {}
    d["tab_words"], d["tab_scales"] = pack_weight(n((K, T)) * s, "e4m3")
    d["tab2_words"], d["tab2_scales"] = pack_weight(n((K, T)) * s, "e4m3")
    d["offs"] = striped(np.random.permutation(T)[:S])
    d["offs2"] = striped(np.random.permutation(T)[:S])
    d["offs3"] = striped(perm[:S])
    d["offs4"] = striped(perm[S:2 * S])
    d["offs5"] = striped(np.random.permutation(T2)[:P])
    d["w1"] = (2.5 * n((K, H)) / s / K**0.5).astype(np.float32)
    d["g1"] = (2.0 * np.exp(0.3 * n(H)) * u[:, 0]).astype(np.float32)
    d["w2_words"], d["w2_scales"] = pack_weight(1.3 * n((K, H)) / s * u.T / K**0.5, "e2m1")
    d["floor2"] = (0.6 * n(H) * u[:, 0]).astype(np.float32)
    d["page0"] = (n((H, T2)) * u).astype(np.float32)
    d["wg1"] = np.exp(0.3 * n((128, S))).astype(np.float32)
    d["wg2"] = np.exp(0.3 * n((128, S))).astype(np.float32)
    d["gx"] = np.exp(0.4 * n(H)).astype(np.float32)
    d["w3"] = (1.2 * n((H, H)) / u / H**0.5).astype(np.float32)
    d["gt"] = (1.2 * np.exp(0.3 * n(H)) * u[:, 0]).astype(np.float32)
    d["w4_words"], d["w4_scales"] = pack_weight(n((H, N)) / u / H**0.5, "e4m3")
    return d

def reference(tab_words, tab_scales, tab2_words, tab2_scales, offs, offs2, offs3, offs4, offs5, w1, g1,
              w2_words, w2_scales, floor2, page0, wg1, wg2, gx, w3, gt, w4_words, w4_scales):
    v = unpack_weight(tab_words, tab_scales, "e4m3")[:, unstriped(offs)]
    v2 = unpack_weight(tab2_words, tab2_scales, "e4m3")[:, unstriped(offs2)]
    h1 = f64(g1)[:, None] / (1.0 + np.exp(-(mxq(f64(w1), 0, "e4m3").T @ v)))
    h2 = np.maximum(unpack_weight(w2_words, w2_scales, "e2m1").T @ v2, f64(floor2)[:, None])
    page = f64(page0).copy()
    page[:, unstriped(offs3)] = np.tile(f64(wg1), (H // 128, 1)) * h1
    page[:, unstriped(offs4)] = np.tile(f64(wg2), (H // 128, 1)) * h2
    seen = page[:, unstriped(offs5)]
    x = mxq(f64(gx)[:, None] * seen, 0, "e4m3")
    y = np.tanh(mxq(f64(w3), 0, "e4m3").T @ x)
    z = mxq(f64(gt)[:, None] * y + seen, 0, "e4m3")
    return unpack_weight(w4_words, w4_scales, "e4m3").T @ z

@@ -1,0 +1,351 @@
+from contextlib import ExitStack
+
+import concourse.mybir as mybir
+
+K, T, S, H, T2, J, N = 1024, 2048, 512, 1024, 2048, 1024, 512
+FLOPS = 2 * (2 * K * H * S + H * H * J + H * N * J)
+
+F32, BF16 = mybir.dt.float32, mybir.dt.bfloat16
+I32, U32, U16, U8 = mybir.dt.int32, mybir.dt.uint32, mybir.dt.uint16, mybir.dt.uint8
+FP8X4, FP4X4 = mybir.dt.float8_e4m3fn_x4, mybir.dt.float4_e2m1fn_x4
+ALU = mybir.AluOpType
+ACT = mybir.ActivationFunctionType
+
+P = 128
+PACK = 4
+KP = P * PACK
+PASSES = 2
+TILES = PASSES * PACK
+CHUNKS = ((0, 512), (512, 1024))
+
+
+def tile_list_tyre_slot_features_kernel(
+    tc, tab_words, tab_scales, tab2_words, tab2_scales, offs, offs2, offs3, offs4, offs5, w1, g1,
+    w2_words, w2_scales, floor2, page0, wg1, wg2, gx, w3, gt, w4_words, w4_scales, out,
+):
+    nc = tc.nc
+    with ExitStack() as ctx:
+        lists = ctx.enter_context(tc.tile_pool(name="lists", bufs=1))
+        sb = ctx.enter_context(tc.tile_pool(name="sb", bufs=1))
+        ps = ctx.enter_context(tc.psum_pool(name="ps", bufs=1))
+
+        def tile(name, cols, dtype, slot=None):
+            return sb.tile([P, cols], dtype, name=name, tag=slot or name, align_bytes=64)
+
+        def bank(name, index, cols):
+            return ps.tile([P, cols], F32, name=name, tag="bank%d" % index)
+
+        def load_list(name, src):
+            dst = lists.tile(list(src.shape), U16, name=name)
+            nc.sync.dma_start(dst[:], src)
+            return dst
+
+        def load_words(name, src, slot):
+            dst = tile(name, src.shape[1], U32, slot)
+            nc.sync.dma_start(out=dst[:].bitcast(I32), in_=src.rearrange("p n i -> p (n i)").bitcast(I32))
+            return dst
+
+        def load_scales_side_by_side(queue, dst, src):
+            for q in range(4):
+                queue.dma_start(
+                    out=dst[32 * q : 32 * q + 4, :].bitcast(I32).rearrange("r (a n) -> r a n", a=PASSES),
+                    in_=src[:, 4 * q : 4 * q + 4, :].rearrange("a r n -> r a n").bitcast(I32),
+                )
+
+        def load_scales_stacked(dst, src):
+            for q in range(4):
+                nc.sync.dma_start(
+                    out=dst[32 * q : 32 * q + 8, :].bitcast(I32), in_=src[:, 4 * q : 4 * q + 4, :].bitcast(I32)
+                )
+
+        def load_channel_vector(name, src):
+            dst = tile(name, TILES, F32)
+            nc.sync.dma_start(
+                out=dst[:].rearrange("p (b t) -> p b t", b=PASSES),
+                in_=src.rearrange("(b p t) -> p b t", b=PASSES, t=PACK),
+            )
+            return dst
+
+        def load_gain(dst, src, t0, t1):
+            rows = src.rearrange("(q t) j -> q (t j)", t=PACK)
+            for q in range(4):
+                nc.sync.dma_start(out=dst[32 * q : 32 * q + 32, t0 * S : t1 * S], in_=rows[:, t0 * S : t1 * S])
+
+        page_rows = page0.rearrange("(b p t) n -> b t p n", b=PASSES, t=PACK)
+        pages = {}
+
+        def load_page(k):
+            pages[k] = tile("page%d" % k, T2, F32)
+            nc.sync.dma_start(out=pages[k][:], in_=page_rows[k // PACK, k % PACK])
+
+        def gather(name, window, offsets, dtype):
+            dst = tile(name, S, dtype)
+            nc.vector.tensor_copy(dst[:], window.indirect(offsets[:]))
+            return dst
+
+        def quantized_weight(name, src, a, b, slot):
+            raw = tile(name + "_raw", PACK * KP, F32, slot)
+            nc.sync.dma_start(
+                out=raw[:].rearrange("p (i c) -> p i c", i=PACK),
+                in_=src[KP * a : KP * (a + 1), KP * b : KP * (b + 1)].rearrange("(p i) c -> p i c", i=PACK),
+            )
+            grouped = tile(name + "_bf16", PACK * KP, BF16, "grouped%d" % ((PASSES * a + b) % 2))
+            nc.scalar.copy(
+                grouped[:].rearrange("p (t m i) -> p m i t", t=PACK, i=PACK),
+                raw[:].rearrange("p (i m t) -> p m i t", i=PACK, t=PACK),
+            )
+            codes = tile(name + "_codes", KP, U32)
+            scales = tile(name + "_scales", KP, U8)
+            nc.vector.quantize_mx(out=codes[:].bitcast(FP8X4), scales=scales[:], in_=grouped[:])
+            return codes, scales
+
+        w2_scales_raw = tile("w2_scales_raw", PASSES * H, U8)
+        v2_table_scales = tile("v2_table_scales", PASSES * T, U8)
+        v_table_scales = tile("v_table_scales", T, U8)
+        w4_planes = tile("w4_planes", N, U8)
+        for plane in (v2_table_scales, w2_scales_raw, v_table_scales, w4_planes):
+            nc.vector.memset(plane[:].bitcast(I32), 0)
+
+        w2_raw = tile("w2_raw", PASSES * 2 * H, U8)
+        nc.sync.dma_start(
+            out=w2_raw[:].bitcast(I32).rearrange("p (a n) -> p a n", a=PASSES),
+            in_=w2_words.rearrange("a p n -> p a n").bitcast(I32),
+        )
+        load_scales_side_by_side(nc.gpsimd, w2_scales_raw, w2_scales)
+        gain2 = tile("gain2", PACK * S, F32)
+        load_gain(gain2, wg2, 0, 1)
+        idx2 = load_list("idx2", offs2)
+        floor_sb = load_channel_vector("floor_sb", floor2)
+        idx4 = load_list("idx4", offs4)
+        load_scales_side_by_side(nc.sync, v2_table_scales, tab2_scales)
+        v2_table = [load_words("v2_table%d" % a, tab2_words[a], "stage%d" % a) for a in range(PASSES)]
+
+        w2_codes = tile("w2_codes", PASSES * 2 * H, U8)
+        w2_planes = tile("w2_planes", PASSES * H, U8)
+        for a in range(PASSES):
+            cols = slice(2 * H * a, 2 * H * (a + 1))
+            nc.vector.tensor_copy(
+                w2_codes[:, cols].rearrange("p (b t m e) -> p b t m e", b=PASSES, t=PACK, e=2),
+                w2_raw[:, cols].rearrange("p (b m t e) -> p b t m e", b=PASSES, t=PACK, e=2),
+            )
+        v2_scales = [
+            gather("v2_scales%d" % a, v2_table_scales[:, T * a : T * (a + 1)], idx2, U8) for a in range(PASSES)
+        ]
+        v2_codes = [gather("v2_codes0", v2_table[0][:], idx2, U32)]
+        nc.vector.tensor_copy(
+            w2_planes[:].rearrange("p (g t m) -> p g t m", t=PACK, m=P),
+            w2_scales_raw[:].rearrange("p (g m t) -> p g t m", t=PACK, m=P),
+        )
+        v2_codes.append(gather("v2_codes1", v2_table[1][:], idx2, U32))
+
+        order2 = [PACK * b + t for t in range(PACK) for b in range(PASSES)]
+        h2 = {}
+        for n, k in enumerate(order2):
+            acc = bank("h2_acc%d" % k, n, S)
+            for a in range(PASSES):
+                nc.tensor.matmul_mx(
+                    out=acc[:],
+                    lhsT=w2_codes[:, 2 * H * a + 2 * P * k : 2 * H * a + 2 * P * (k + 1)].bitcast(FP4X4),
+                    lhsT_scale=w2_planes[:, H * a + P * k : H * a + P * (k + 1)],
+                    rhs=v2_codes[a][:].bitcast(FP8X4),
+                    rhs_scale=v2_scales[a][:],
+                    start=(a == 0),
+                    stop=(a == PASSES - 1),
+                )
+            summed = acc
+            if n > 0:
+                summed = tile("h2_sum%d" % k, S, F32, "spill%d" % (n % 2))
+                nc.scalar.copy(summed[:], acc[:])
+            h2[k] = tile("h2_%d" % k, S, F32, "h%d" % k)
+            nc.vector.tensor_scalar(h2[k][:], summed[:], floor_sb[:, k : k + 1], None, ALU.max)
+
+        def scatter(k, offsets, values, gain):
+            t = k % PACK
+            nc.vector.tensor_tensor(
+                pages[k][:].indirect(offsets[:]), values[:], gain[:, S * t : S * (t + 1)], ALU.mult
+            )
+
+        def put_h2(n):
+            load_page(order2[n])
+            scatter(order2[n], idx4, h2[order2[n]], gain2)
+
+        put_h2(0)
+        put_h2(1)
+        load_gain(gain2, wg2, 1, PACK)
+        put_h2(2)
+        idx = load_list("idx", offs)
+        load_scales_stacked(v_table_scales, tab_scales)
+        v_scales = gather("v_scales", v_table_scales[:], idx, U8)
+        v_codes = []
+        for a in range(PASSES):
+            table = load_words("v_table%d" % a, tab_words[a], "stage%d" % (2 + a))
+            v_codes.append(gather("v_codes%d" % a, table[:], idx, U32))
+            put_h2(3 + a)
+        g1_sb = load_channel_vector("g1_sb", g1)
+        w1q = {}
+        for a in range(PASSES):
+            w1q[a, 0] = quantized_weight("w1_%d0" % a, w1, a, 0, "stage%d" % a)
+            put_h2(5 + a)
+
+        h1 = {}
+
+        def make_h1(b):
+            for t in range(PACK):
+                k = PACK * b + t
+                acc = bank("h1_acc%d" % k, k, S)
+                for a in range(PASSES):
+                    codes, scales = w1q[a, b]
+                    nc.tensor.matmul_mx(
+                        out=acc[:],
+                        lhsT=codes[:, P * t : P * (t + 1)].bitcast(FP8X4),
+                        lhsT_scale=scales[:, P * t : P * (t + 1)],
+                        rhs=v_codes[a][:].bitcast(FP8X4),
+                        rhs_scale=v_scales[4 * a :, :],
+                        start=(a == 0),
+                        stop=(a == PASSES - 1),
+                    )
+                gate = tile("gate%d" % k, S, F32, "spill%d" % (k % 2))
+                nc.scalar.activation(gate[:], acc[:], ACT.Sigmoid)
+                if k == TILES - 1:
+                    h1[k] = gate
+                else:
+                    h1[k] = tile("h1_%d" % k, S, F32, "h%d" % k)
+                    nc.scalar.activation(h1[k][:], gate[:], ACT.Copy, scale=g1_sb[:, k : k + 1])
+
+        make_h1(0)
+        put_h2(7)
+        for a in range(PASSES):
+            w1q[a, 1] = quantized_weight("w1_%d1" % a, w1, a, 1, "stage%d" % (2 + a))
+        make_h1(1)
+        idx3 = load_list("idx3", offs3)
+        idx5 = load_list("idx5", offs5)
+        gx_sb = load_channel_vector("gx_sb", gx)
+        gt_sb = load_channel_vector("gt_sb", gt)
+        gain1 = tile("gain1", PACK * S, F32)
+        load_gain(gain1, wg1, 0, PACK)
+
+        w3q = {}
+        x_bf16 = [tile("x_bf16_0", PACK * J, BF16, "gain2")]
+        x_codes = [tile("x_codes0", J, U32, "w2_raw"), tile("x_codes1", J, U32, "w2_codes")]
+        x_scales = [tile("x_scales%d" % a, J, U8) for a in range(PASSES)]
+        seen = {}
+
+        def read_page(k, c0, c1):
+            a, t = divmod(k, PACK)
+            nc.vector.tensor_copy(seen[k][:, c0:c1], pages[k][:].indirect(idx5[:, c0 // 16 : c1 // 16]))
+            nc.scalar.activation(
+                x_bf16[a][:, PACK * c0 + t : PACK * c1 : PACK], seen[k][:, c0:c1], ACT.Copy, scale=gx_sb[:, k : k + 1]
+            )
+
+        def quantize_x(a, c0, c1):
+            nc.vector.quantize_mx(
+                out=x_codes[a][:, c0:c1].bitcast(FP8X4),
+                scales=x_scales[a][:, c0:c1],
+                in_=x_bf16[a][:, PACK * c0 : PACK * c1],
+            )
+
+        for k in range(TILES):
+            if k == TILES - 1:
+                gate = h1[k]
+                h1[k] = tile("h1_%d" % k, S, F32, "gain2")
+                nc.vector.tensor_scalar(h1[k][:], gate[:], g1_sb[:, k : k + 1], None, ALU.mult)
+            scatter(k, idx3, h1[k], gain1)
+            seen[k] = tile("seen%d" % k, J, F32)
+            if k < TILES - 1:
+                read_page(k, 0, J)
+            if k == PACK - 1:
+                quantize_x(0, 0, J)
+            if k < PACK:
+                a, b = divmod(k, PASSES)
+                w3q[a, b] = quantized_weight("w3_%d%d" % (a, b), w3, a, b, "stage%d" % k)
+            if k == PACK - 1:
+                x_bf16.append(tile("x_bf16_1", PACK * J, BF16, "stage3"))
+                w4_codes = tile("w4_codes", PASSES * N, U32)
+                nc.sync.dma_start(
+                    out=w4_codes[:].bitcast(I32).rearrange("p (a n) -> p a n", a=PASSES),
+                    in_=w4_words.rearrange("a p n i -> p a (n i)").bitcast(I32),
+                )
+                load_scales_stacked(w4_planes, w4_scales)
+        for c0, c1 in CHUNKS:
+            read_page(TILES - 1, c0, c1)
+        for c0, c1 in CHUNKS:
+            quantize_x(1, c0, c1)
+
+        def product3(acc, k, a, c0, c1):
+            b, t = divmod(k, PACK)
+            codes, scales = w3q[a, b]
+            nc.tensor.matmul_mx(
+                out=acc[:],
+                lhsT=codes[:, P * t : P * (t + 1)].bitcast(FP8X4),
+                lhsT_scale=scales[:, P * t : P * (t + 1)],
+                rhs=x_codes[a][:, c0:c1].bitcast(FP8X4),
+                rhs_scale=x_scales[a][:, c0:c1],
+                start=(a == 0),
+                stop=(a == PASSES - 1),
+            )
+
+        y_ring = [tile("y_ring%d" % i, PACK * 512, F32, "stage%d" % i) for i in range(PASSES)]
+        z_flat = tile("z_flat", TILES * 512, BF16, "stage2")
+        z_bf16 = tile("z_bf16", TILES * 512, BF16, "page0")
+        z_codes = tile("z_codes", PASSES * J, U32, "page1")
+        z_scales = tile("z_scales", PASSES * J, U8, "v_table_scales")
+        staged = [tile("staged%d" % i, PACK * 512, F32, "page%d" % (2 + i)) for i in range(2)]
+
+        def make_z(c, c0, c1):
+            width = c1 - c0
+            accs = [bank("y_acc%d_%d" % (c, k), k if c == 0 else k % 4, width) for k in range(TILES)] if c == 0 else {}
+            if c == 0:
+                for k in range(TILES):
+                    product3(accs[k], k, 0, c0, c1)
+            for k in range(TILES):
+                b, t = divmod(k, PACK)
+                if c > 0:
+                    accs[k] = bank("y_acc%d_%d" % (c, k), k % 4, width)
+                    product3(accs[k], k, 0, c0, c1)
+                product3(accs[k], k, 1, c0, c1)
+                y = y_ring[b][:, 512 * t : 512 * t + width]
+                nc.scalar.activation(y, accs[k][:], ACT.Tanh)
+                flat = z_flat[:, PACK * 512 * b : PACK * 512 * b + PACK * width]
+                nc.vector.scalar_tensor_tensor(
+                    flat[:, width * t : width * (t + 1)], y, gt_sb[:, k : k + 1], seen[k][:, c0:c1], ALU.mult, ALU.add
+                )
+                if t == PACK - 1:
+                    woven = z_bf16[:, PACK * 512 * b : PACK * 512 * b + PACK * width]
+                    nc.vector.tensor_copy(
+                        woven.rearrange("p (c i t) -> p c t i", i=4, t=PACK),
+                        flat.rearrange("p (t c i) -> p c t i", i=4, t=PACK),
+                    )
+                    nc.vector.quantize_mx(
+                        out=z_codes[:, J * b + c0 : J * b + c1].bitcast(FP8X4),
+                        scales=z_scales[:, J * b + c0 : J * b + c1],
+                        in_=woven,
+                    )
+
+        def make_out(c, c0, c1):
+            width = c1 - c0
+            accs = [bank("out_acc%d_%d" % (c, n), 4 + n, width) for n in range(N // P)]
+            for a in range(PASSES):
+                for n in range(N // P):
+                    nc.tensor.matmul_mx(
+                        out=accs[n][:],
+                        lhsT=w4_codes[:, N * a + P * n : N * a + P * (n + 1)].bitcast(FP8X4),
+                        lhsT_scale=w4_planes[4 * a :, P * n : P * (n + 1)],
+                        rhs=z_codes[:, J * a + c0 : J * a + c1].bitcast(FP8X4),
+                        rhs_scale=z_scales[:, J * a + c0 : J * a + c1],
+                        start=(a == 0),
+                        stop=(a == PASSES - 1),
+                    )
+            last = c == len(CHUNKS) - 1
+            for n in range(N // P):
+                result = staged[c % 2][:, 512 * n : 512 * n + width]
+                if last and n % 2 == 1:
+                    nc.vector.tensor_copy(result, accs[n][:])
+                else:
+                    nc.scalar.copy(result, accs[n][:])
+                nc.sync.dma_start(out=out[P * n : P * (n + 1), c0:c1], in_=result)
+
+        for c, (c0, c1) in enumerate(CHUNKS):
+            make_z(c, c0, c1)
+            if c > 0:
+                make_out(c - 1, *CHUNKS[c - 1])
+        make_out(len(CHUNKS) - 1, *CHUNKS[-1])

@@ -16,7 +16,7 @@ PACK = 4
 KP = P * PACK
 PASSES = 2
 TILES = PASSES * PACK
-CHUNKS = ((0, 512), (512, 1024))
+CHUNKS = ((0, 256), (256, 768), (768, 1024))
 
 
 def tile_list_tyre_slot_features_kernel(
@@ -83,18 +83,18 @@ def tile_list_tyre_slot_features_kernel(
             nc.vector.tensor_copy(dst[:], window.indirect(offsets[:]))
             return dst
 
-        def quantized_weight(name, src, a, b, slot):
+        def quantized_weight(name, src, a, b, slot, turn, codes_slot=None):
             raw = tile(name + "_raw", PACK * KP, F32, slot)
             nc.sync.dma_start(
                 out=raw[:].rearrange("p (i c) -> p i c", i=PACK),
                 in_=src[KP * a : KP * (a + 1), KP * b : KP * (b + 1)].rearrange("(p i) c -> p i c", i=PACK),
             )
-            grouped = tile(name + "_bf16", PACK * KP, BF16, "grouped%d" % ((PASSES * a + b) % 2))
+            grouped = tile(name + "_bf16", PACK * KP, BF16, "grouped%d" % turn)
             nc.scalar.copy(
                 grouped[:].rearrange("p (t m i) -> p m i t", t=PACK, i=PACK),
                 raw[:].rearrange("p (i m t) -> p m i t", i=PACK, t=PACK),
             )
-            codes = tile(name + "_codes", KP, U32)
+            codes = tile(name + "_codes", KP, U32, codes_slot)
             scales = tile(name + "_scales", KP, U8)
             nc.vector.quantize_mx(out=codes[:].bitcast(FP8X4), scales=scales[:], in_=grouped[:])
             return codes, scales
@@ -120,14 +120,16 @@ def tile_list_tyre_slot_features_kernel(
         load_scales_side_by_side(nc.sync, v2_table_scales, tab2_scales)
         v2_table = [load_words("v2_table%d" % a, tab2_words[a], "stage%d" % a) for a in range(PASSES)]
 
-        w2_codes = tile("w2_codes", PASSES * 2 * H, U8)
-        w2_planes = tile("w2_planes", PASSES * H, U8)
-        for a in range(PASSES):
-            cols = slice(2 * H * a, 2 * H * (a + 1))
+        def deal_w2_codes(b, slot):
+            dealt = tile("w2_codes%d" % b, 2 * H, U8, slot)
             nc.vector.tensor_copy(
-                w2_codes[:, cols].rearrange("p (b t m e) -> p b t m e", b=PASSES, t=PACK, e=2),
-                w2_raw[:, cols].rearrange("p (b m t e) -> p b t m e", b=PASSES, t=PACK, e=2),
+                dealt[:].rearrange("p (a t m e) -> p a t m e", a=PASSES, t=PACK, e=2),
+                w2_raw[:].rearrange("p (a b m t e) -> p b a t m e", a=PASSES, b=PASSES, t=PACK, e=2)[:, b],
             )
+            return dealt
+
+        w2_codes = [deal_w2_codes(0, None)]
+        w2_planes = tile("w2_planes", PASSES * H, U8)
         v2_scales = [
             gather("v2_scales%d" % a, v2_table_scales[:, T * a : T * (a + 1)], idx2, U8) for a in range(PASSES)
         ]
@@ -137,27 +139,22 @@ def tile_list_tyre_slot_features_kernel(
             w2_scales_raw[:].rearrange("p (g m t) -> p g t m", t=PACK, m=P),
         )
         v2_codes.append(gather("v2_codes1", v2_table[1][:], idx2, U32))
+        w2_codes.append(deal_w2_codes(1, "stage1"))
 
         order2 = [PACK * b + t for t in range(PACK) for b in range(PASSES)]
-        h2 = {}
+        h2_acc = {}
         for n, k in enumerate(order2):
-            acc = bank("h2_acc%d" % k, n, S)
+            acc = h2_acc[k] = bank("h2_acc%d" % k, n, S)
             for a in range(PASSES):
                 nc.tensor.matmul_mx(
                     out=acc[:],
-                    lhsT=w2_codes[:, 2 * H * a + 2 * P * k : 2 * H * a + 2 * P * (k + 1)].bitcast(FP4X4),
+                    lhsT=w2_codes[k // PACK][:, H * a + 2 * P * (k % PACK) : H * a + 2 * P * (k % PACK + 1)].bitcast(FP4X4),
                     lhsT_scale=w2_planes[:, H * a + P * k : H * a + P * (k + 1)],
                     rhs=v2_codes[a][:].bitcast(FP8X4),
                     rhs_scale=v2_scales[a][:],
                     start=(a == 0),
                     stop=(a == PASSES - 1),
                 )
-            summed = acc
-            if n > 0:
-                summed = tile("h2_sum%d" % k, S, F32, "spill%d" % (n % 2))
-                nc.scalar.copy(summed[:], acc[:])
-            h2[k] = tile("h2_%d" % k, S, F32, "h%d" % k)
-            nc.vector.tensor_scalar(h2[k][:], summed[:], floor_sb[:, k : k + 1], None, ALU.max)
 
         def scatter(k, offsets, values, gain):
             t = k % PACK
@@ -165,9 +162,18 @@ def tile_list_tyre_slot_features_kernel(
                 pages[k][:].indirect(offsets[:]), values[:], gain[:, S * t : S * (t + 1)], ALU.mult
             )
 
+        h2_slots = ["h0", "v_scales", "v_codes", "grouped0", "grouped1", "h1", "grouped0", "grouped1"]
+
         def put_h2(n):
-            load_page(order2[n])
-            scatter(order2[n], idx4, h2[order2[n]], gain2)
+            k = order2[n]
+            load_page(k)
+            summed = h2_acc[k]
+            if n > 0:
+                summed = tile("h2_sum%d" % k, S, F32, "spill%d" % (n % 2))
+                nc.scalar.copy(summed[:], h2_acc[k][:])
+            h2 = tile("h2_%d" % k, S, F32, h2_slots[n])
+            nc.vector.tensor_scalar(h2[:], summed[:], floor_sb[:, k : k + 1], None, ALU.max)
+            scatter(k, idx4, h2, gain2)
 
         put_h2(0)
         put_h2(1)
@@ -176,16 +182,17 @@ def tile_list_tyre_slot_features_kernel(
         idx = load_list("idx", offs)
         load_scales_stacked(v_table_scales, tab_scales)
         v_scales = gather("v_scales", v_table_scales[:], idx, U8)
-        v_codes = []
+        v_codes = tile("v_codes", PASSES * S, U32)
         for a in range(PASSES):
             table = load_words("v_table%d" % a, tab_words[a], "stage%d" % (2 + a))
-            v_codes.append(gather("v_codes%d" % a, table[:], idx, U32))
+            nc.vector.tensor_copy(v_codes[:, S * a : S * (a + 1)], table[:].indirect(idx[:]))
             put_h2(3 + a)
         g1_sb = load_channel_vector("g1_sb", g1)
         w1q = {}
+        put_h2(5)
         for a in range(PASSES):
-            w1q[a, 0] = quantized_weight("w1_%d0" % a, w1, a, 0, "stage%d" % a)
-            put_h2(5 + a)
+            w1q[a, 0] = quantized_weight("w1_%d0" % a, w1, a, 0, "stage%d" % a, a)
+            put_h2(6 + a)
 
         h1 = {}
 
@@ -199,12 +206,12 @@ def tile_list_tyre_slot_features_kernel(
                         out=acc[:],
                         lhsT=codes[:, P * t : P * (t + 1)].bitcast(FP8X4),
                         lhsT_scale=scales[:, P * t : P * (t + 1)],
-                        rhs=v_codes[a][:].bitcast(FP8X4),
+                        rhs=v_codes[:, S * a : S * (a + 1)].bitcast(FP8X4),
                         rhs_scale=v_scales[4 * a :, :],
                         start=(a == 0),
                         stop=(a == PASSES - 1),
                     )
-                gate = tile("gate%d" % k, S, F32, "spill%d" % (k % 2))
+                gate = tile("gate%d" % k, S, F32, ("grouped%d" if k in (2, 3) else "spill%d") % (k % 2))
                 nc.scalar.activation(gate[:], acc[:], ACT.Sigmoid)
                 if k == TILES - 1:
                     h1[k] = gate
@@ -213,9 +220,8 @@ def tile_list_tyre_slot_features_kernel(
                     nc.scalar.activation(h1[k][:], gate[:], ACT.Copy, scale=g1_sb[:, k : k + 1])
 
         make_h1(0)
-        put_h2(7)
         for a in range(PASSES):
-            w1q[a, 1] = quantized_weight("w1_%d1" % a, w1, a, 1, "stage%d" % (2 + a))
+            w1q[a, 1] = quantized_weight("w1_%d1" % a, w1, a, 1, "stage%d" % (2 + a), a)
         make_h1(1)
         idx3 = load_list("idx3", offs3)
         idx5 = load_list("idx5", offs5)
@@ -225,8 +231,8 @@ def tile_list_tyre_slot_features_kernel(
         load_gain(gain1, wg1, 0, PACK)
 
         w3q = {}
-        x_bf16 = [tile("x_bf16_0", PACK * J, BF16, "gain2")]
-        x_codes = [tile("x_codes0", J, U32, "w2_raw"), tile("x_codes1", J, U32, "w2_codes")]
+        x_bf16 = [tile("x_bf16_0", PACK * J, BF16, "gain2"), tile("x_bf16_1", PACK * J, BF16)]
+        x_codes = [tile("x_codes0", J, U32, "w2_raw"), tile("x_codes1", J, U32, "v2_table_scales")]
         x_scales = [tile("x_scales%d" % a, J, U8) for a in range(PASSES)]
         seen = {}
 
@@ -255,11 +261,10 @@ def tile_list_tyre_slot_features_kernel(
                 read_page(k, 0, J)
             if k == PACK - 1:
                 quantize_x(0, 0, J)
-            if k < PACK:
-                a, b = divmod(k, PASSES)
-                w3q[a, b] = quantized_weight("w3_%d%d" % (a, b), w3, a, b, "stage%d" % k)
-            if k == PACK - 1:
-                x_bf16.append(tile("x_bf16_1", PACK * J, BF16, "stage3"))
+            if 1 <= k <= PACK:
+                a, b = divmod(k - 1, PASSES)
+                w3q[a, b] = quantized_weight("w3_%d%d" % (a, b), w3, a, b, "stage%d" % (k - 1), b, "h%d" % k)
+            if k == PACK:
                 w4_codes = tile("w4_codes", PASSES * N, U32)
                 nc.sync.dma_start(
                     out=w4_codes[:].bitcast(I32).rearrange("p (a n) -> p a n", a=PASSES),
@@ -285,33 +290,34 @@ def tile_list_tyre_slot_features_kernel(
             )
 
         y_ring = [tile("y_ring%d" % i, PACK * 512, F32, "stage%d" % i) for i in range(PASSES)]
-        z_flat = tile("z_flat", TILES * 512, BF16, "stage2")
-        z_bf16 = tile("z_bf16", TILES * 512, BF16, "page0")
+        z_flat = [tile("z_flat%d" % b, PACK * J, BF16, "stage%d" % (2 + b)) for b in range(PASSES)]
+        z_bf16 = [tile("z_bf16_%d" % b, PACK * J, BF16, "page%d" % (4 * b)) for b in range(PASSES)]
         z_codes = tile("z_codes", PASSES * J, U32, "page1")
         z_scales = tile("z_scales", PASSES * J, U8, "v_table_scales")
         staged = [tile("staged%d" % i, PACK * 512, F32, "page%d" % (2 + i)) for i in range(2)]
 
         def make_z(c, c0, c1):
             width = c1 - c0
-            accs = [bank("y_acc%d_%d" % (c, k), k if c == 0 else k % 4, width) for k in range(TILES)] if c == 0 else {}
+            accs = [bank("y_acc%d_%d" % (c, k), k, width) for k in range(TILES)] if c == 0 else {}
             if c == 0:
                 for k in range(TILES):
                     product3(accs[k], k, 0, c0, c1)
             for k in range(TILES):
                 b, t = divmod(k, PACK)
                 if c > 0:
-                    accs[k] = bank("y_acc%d_%d" % (c, k), k % 4, width)
+                    accs[k] = bank("y_acc%d_%d" % (c, k), k if c == 1 else k % 4, width)
                     product3(accs[k], k, 0, c0, c1)
                 product3(accs[k], k, 1, c0, c1)
                 y = y_ring[b][:, 512 * t : 512 * t + width]
                 nc.scalar.activation(y, accs[k][:], ACT.Tanh)
-                flat = z_flat[:, PACK * 512 * b : PACK * 512 * b + PACK * width]
+                flat = z_flat[b][:, PACK * c0 : PACK * c1]
                 nc.vector.scalar_tensor_tensor(
                     flat[:, width * t : width * (t + 1)], y, gt_sb[:, k : k + 1], seen[k][:, c0:c1], ALU.mult, ALU.add
                 )
                 if t == PACK - 1:
-                    woven = z_bf16[:, PACK * 512 * b : PACK * 512 * b + PACK * width]
-                    nc.vector.tensor_copy(
+                    woven = z_bf16[b][:, PACK * c0 : PACK * c1]
+                    weave = nc.scalar.copy if (c, b) == (1, 0) else nc.vector.tensor_copy
+                    weave(
                         woven.rearrange("p (c i t) -> p c t i", i=4, t=PACK),
                         flat.rearrange("p (t c i) -> p c t i", i=4, t=PACK),
                     )

@@ -66,9 +66,9 @@ def tile_list_tyre_slot_features_kernel(
             )
             return dst
 
-        def load_gain(dst, src, t0, t1):
+        def load_gain(dst, src, t0, t1, quadrants=range(4)):
             rows = src.rearrange("(q t) j -> q (t j)", t=PACK)
-            for q in range(4):
+            for q in quadrants:
                 nc.sync.dma_start(out=dst[32 * q : 32 * q + 32, t0 * S : t1 * S], in_=rows[:, t0 * S : t1 * S])
 
         page_rows = page0.rearrange("(b p t) n -> b t p n", b=PASSES, t=PACK)
@@ -106,40 +106,45 @@ def tile_list_tyre_slot_features_kernel(
         for plane in (v2_table_scales, w2_scales_raw, v_table_scales, w4_planes):
             nc.vector.memset(plane[:].bitcast(I32), 0)
 
+        idx2 = load_list("idx2", offs2)
+        floor_sb = load_channel_vector("floor_sb", floor2)
+        idx4 = load_list("idx4", offs4)
+        gain2 = tile("gain2", PACK * S, F32)
+        load_gain(gain2, wg2, 0, 1, (0,))
         w2_raw = tile("w2_raw", PASSES * 2 * H, U8)
         nc.sync.dma_start(
             out=w2_raw[:].bitcast(I32).rearrange("p (a n) -> p a n", a=PASSES),
             in_=w2_words.rearrange("a p n -> p a n").bitcast(I32),
         )
-        load_scales_side_by_side(nc.gpsimd, w2_scales_raw, w2_scales)
-        gain2 = tile("gain2", PACK * S, F32)
-        load_gain(gain2, wg2, 0, 1)
-        idx2 = load_list("idx2", offs2)
-        floor_sb = load_channel_vector("floor_sb", floor2)
-        idx4 = load_list("idx4", offs4)
+        v2_table = [load_words("v2_table0", tab2_words[0], "stage0")]
+        load_gain(gain2, wg2, 0, 1, (1, 2))
         load_scales_side_by_side(nc.sync, v2_table_scales, tab2_scales)
-        v2_table = [load_words("v2_table%d" % a, tab2_words[a], "stage%d" % a) for a in range(PASSES)]
+        v2_table.append(load_words("v2_table1", tab2_words[1], "stage1"))
+        load_scales_side_by_side(nc.sync, w2_scales_raw, w2_scales)
+        load_gain(gain2, wg2, 0, 1, (3,))
 
-        def deal_w2_codes(b, slot):
-            dealt = tile("w2_codes%d" % b, 2 * H, U8, slot)
+        w2_codes = tile("w2_codes", PASSES * 2 * H, U8)
+        for a in range(PASSES):
+            cols = slice(2 * H * a, 2 * H * (a + 1))
             nc.vector.tensor_copy(
-                dealt[:].rearrange("p (a t m e) -> p a t m e", a=PASSES, t=PACK, e=2),
-                w2_raw[:].rearrange("p (a b m t e) -> p b a t m e", a=PASSES, b=PASSES, t=PACK, e=2)[:, b],
+                w2_codes[:, cols].rearrange("p (b t m e) -> p b t m e", b=PASSES, t=PACK, e=2),
+                w2_raw[:, cols].rearrange("p (b m t e) -> p b t m e", b=PASSES, t=PACK, e=2),
+            )
+
+        def deal_w2_scales(b, slot):
+            dealt = tile("w2_planes%d" % b, H, U8, slot)
+            nc.vector.tensor_copy(
+                dealt[:].rearrange("p (a t m) -> p a t m", a=PASSES, t=PACK),
+                w2_scales_raw[:].rearrange("p (a b m t) -> p b a t m", a=PASSES, b=PASSES, t=PACK)[:, b],
             )
             return dealt
 
-        w2_codes = [deal_w2_codes(0, None)]
-        w2_planes = tile("w2_planes", PASSES * H, U8)
+        v2_codes = [gather("v2_codes0", v2_table[0][:], idx2, U32)]
         v2_scales = [
             gather("v2_scales%d" % a, v2_table_scales[:, T * a : T * (a + 1)], idx2, U8) for a in range(PASSES)
         ]
-        v2_codes = [gather("v2_codes0", v2_table[0][:], idx2, U32)]
-        nc.vector.tensor_copy(
-            w2_planes[:].rearrange("p (g t m) -> p g t m", t=PACK, m=P),
-            w2_scales_raw[:].rearrange("p (g m t) -> p g t m", t=PACK, m=P),
-        )
         v2_codes.append(gather("v2_codes1", v2_table[1][:], idx2, U32))
-        w2_codes.append(deal_w2_codes(1, "stage1"))
+        w2_planes = [deal_w2_scales(0, None), deal_w2_scales(1, "stage1")]
 
         order2 = [PACK * b + t for t in range(PACK) for b in range(PASSES)]
         h2_acc = {}
@@ -148,8 +153,8 @@ def tile_list_tyre_slot_features_kernel(
             for a in range(PASSES):
                 nc.tensor.matmul_mx(
                     out=acc[:],
-                    lhsT=w2_codes[k // PACK][:, H * a + 2 * P * (k % PACK) : H * a + 2 * P * (k % PACK + 1)].bitcast(FP4X4),
-                    lhsT_scale=w2_planes[:, H * a + P * k : H * a + P * (k + 1)],
+                    lhsT=w2_codes[:, 2 * H * a + 2 * P * k : 2 * H * a + 2 * P * (k + 1)].bitcast(FP4X4),
+                    lhsT_scale=w2_planes[k // PACK][:, KP * a + P * (k % PACK) : KP * a + P * (k % PACK + 1)],
                     rhs=v2_codes[a][:].bitcast(FP8X4),
                     rhs_scale=v2_scales[a][:],
                     start=(a == 0),
@@ -221,7 +226,7 @@ def tile_list_tyre_slot_features_kernel(
 
         make_h1(0)
         for a in range(PASSES):
-            w1q[a, 1] = quantized_weight("w1_%d1" % a, w1, a, 1, "stage%d" % (2 + a), a)
+            w1q[a, 1] = quantized_weight("w1_%d1" % a, w1, a, 1, "stage%d" % (2 + a), a, "h%d" % a)
         make_h1(1)
         idx3 = load_list("idx3", offs3)
         idx5 = load_list("idx5", offs5)
@@ -263,7 +268,7 @@ def tile_list_tyre_slot_features_kernel(
                 quantize_x(0, 0, J)
             if 1 <= k <= PACK:
                 a, b = divmod(k - 1, PASSES)
-                w3q[a, b] = quantized_weight("w3_%d%d" % (a, b), w3, a, b, "stage%d" % (k - 1), b, "h%d" % k)
+                w3q[a, b] = quantized_weight("w3_%d%d" % (a, b), w3, a, b, "stage%d" % (k - 1), b, "h%d" % (k + 1))
             if k == PACK:
                 w4_codes = tile("w4_codes", PASSES * N, U32)
                 nc.sync.dma_start(

@@ -66,7 +66,7 @@ def tile_list_tyre_slot_features_kernel(
             )
             return dst
 
-        def load_gain(dst, src, t0, t1, quadrants=range(4)):
+        def load_gain(dst, src, t0, t1, quadrants=(0, 2, 1, 3)):
             rows = src.rearrange("(q t) j -> q (t j)", t=PACK)
             for q in quadrants:
                 nc.sync.dma_start(out=dst[32 * q : 32 * q + 32, t0 * S : t1 * S], in_=rows[:, t0 * S : t1 * S])
@@ -83,17 +83,20 @@ def tile_list_tyre_slot_features_kernel(
             nc.vector.tensor_copy(dst[:], window.indirect(offsets[:]))
             return dst
 
-        def quantized_weight(name, src, a, b, slot, turn, codes_slot=None):
-            raw = tile(name + "_raw", PACK * KP, F32, slot)
+        def rounded_weight(name, src, a, b, stage, turn):
+            raw = tile(name + "_raw", PACK * KP, F32, "stage%d" % stage)
             nc.sync.dma_start(
                 out=raw[:].rearrange("p (i c) -> p i c", i=PACK),
                 in_=src[KP * a : KP * (a + 1), KP * b : KP * (b + 1)].rearrange("(p i) c -> p i c", i=PACK),
             )
             grouped = tile(name + "_bf16", PACK * KP, BF16, "grouped%d" % turn)
-            nc.scalar.copy(
-                grouped[:].rearrange("p (t m i) -> p m i t", t=PACK, i=PACK),
-                raw[:].rearrange("p (i m t) -> p m i t", i=PACK, t=PACK),
-            )
+            dst = grouped[:].rearrange("p (t m i) -> p m t i", t=PACK, i=PACK)
+            src_view = raw[:].rearrange("p (i m t) -> p m t i", i=PACK, t=PACK)
+            for t in (0, 2):
+                nc.scalar.copy(dst[:, :, t : t + 2, :], src_view[:, :, t : t + 2, :])
+            return grouped
+
+        def quantized(name, grouped, codes_slot=None):
             codes = tile(name + "_codes", KP, U32, codes_slot)
             scales = tile(name + "_scales", KP, U8)
             nc.vector.quantize_mx(out=codes[:].bitcast(FP8X4), scales=scales[:], in_=grouped[:])
@@ -117,7 +120,7 @@ def tile_list_tyre_slot_features_kernel(
             in_=w2_words.rearrange("a p n -> p a n").bitcast(I32),
         )
         v2_table = [load_words("v2_table0", tab2_words[0], "stage0")]
-        load_gain(gain2, wg2, 0, 1, (1, 2))
+        load_gain(gain2, wg2, 0, 1, (2, 1))
         load_scales_side_by_side(nc.sync, v2_table_scales, tab2_scales)
         v2_table.append(load_words("v2_table1", tab2_words[1], "stage1"))
         load_scales_side_by_side(nc.sync, w2_scales_raw, w2_scales)
@@ -167,7 +170,7 @@ def tile_list_tyre_slot_features_kernel(
                 pages[k][:].indirect(offsets[:]), values[:], gain[:, S * t : S * (t + 1)], ALU.mult
             )
 
-        h2_slots = ["h0", "v_scales", "v_codes", "grouped0", "grouped1", "h1", "grouped0", "grouped1"]
+        h2_slots = ["h0", "v_scales", "v_codes", "h1", "w1_00_codes", "w1_10_codes", "grouped0", "grouped1"]
 
         def put_h2(n):
             k = order2[n]
@@ -191,13 +194,17 @@ def tile_list_tyre_slot_features_kernel(
         for a in range(PASSES):
             table = load_words("v_table%d" % a, tab_words[a], "stage%d" % (2 + a))
             nc.vector.tensor_copy(v_codes[:, S * a : S * (a + 1)], table[:].indirect(idx[:]))
-            put_h2(3 + a)
+            if a == 0:
+                put_h2(3)
         g1_sb = load_channel_vector("g1_sb", g1)
         w1q = {}
-        put_h2(5)
         for a in range(PASSES):
-            w1q[a, 0] = quantized_weight("w1_%d0" % a, w1, a, 0, "stage%d" % a, a)
-            put_h2(6 + a)
+            rounded = rounded_weight("w1_%d0" % a, w1, a, 0, a, a)
+            put_h2(4 + a)
+            w1q[a, 0] = quantized("w1_%d0" % a, rounded)
+        w1_01 = rounded_weight("w1_01", w1, 0, 1, 2, 2)
+        put_h2(6)
+        put_h2(7)
 
         h1 = {}
 
@@ -216,7 +223,7 @@ def tile_list_tyre_slot_features_kernel(
                         start=(a == 0),
                         stop=(a == PASSES - 1),
                     )
-                gate = tile("gate%d" % k, S, F32, ("grouped%d" if k in (2, 3) else "spill%d") % (k % 2))
+                gate = tile("gate%d" % k, S, F32, "grouped3" if k == PACK - 1 else "spill%d" % (k % 2))
                 nc.scalar.activation(gate[:], acc[:], ACT.Sigmoid)
                 if k == TILES - 1:
                     h1[k] = gate
@@ -225,8 +232,8 @@ def tile_list_tyre_slot_features_kernel(
                     nc.scalar.activation(h1[k][:], gate[:], ACT.Copy, scale=g1_sb[:, k : k + 1])
 
         make_h1(0)
-        for a in range(PASSES):
-            w1q[a, 1] = quantized_weight("w1_%d1" % a, w1, a, 1, "stage%d" % (2 + a), a, "h%d" % a)
+        w1q[0, 1] = quantized("w1_01", w1_01, "h0")
+        w1q[1, 1] = quantized("w1_11", rounded_weight("w1_11", w1, 1, 1, 3, 3), "h1")
         make_h1(1)
         idx3 = load_list("idx3", offs3)
         idx5 = load_list("idx5", offs5)
@@ -240,13 +247,18 @@ def tile_list_tyre_slot_features_kernel(
         x_codes = [tile("x_codes0", J, U32, "w2_raw"), tile("x_codes1", J, U32, "v2_table_scales")]
         x_scales = [tile("x_scales%d" % a, J, U8) for a in range(PASSES)]
         seen = {}
+        x_flat = []
 
         def read_page(k, c0, c1):
             a, t = divmod(k, PACK)
             nc.vector.tensor_copy(seen[k][:, c0:c1], pages[k][:].indirect(idx5[:, c0 // 16 : c1 // 16]))
-            nc.scalar.activation(
-                x_bf16[a][:, PACK * c0 + t : PACK * c1 : PACK], seen[k][:, c0:c1], ACT.Copy, scale=gx_sb[:, k : k + 1]
-            )
+            if k == 0:
+                x_flat.append(tile("x_flat", PACK * J, BF16, "page0"))
+            if a == 0:
+                dst = x_flat[0][:, J * t : J * (t + 1)]
+            else:
+                dst = x_bf16[a][:, PACK * c0 + t : PACK * c1 : PACK]
+            nc.scalar.activation(dst, seen[k][:, c0:c1], ACT.Copy, scale=gx_sb[:, k : k + 1])
 
         def quantize_x(a, c0, c1):
             nc.vector.quantize_mx(
@@ -265,10 +277,15 @@ def tile_list_tyre_slot_features_kernel(
             if k < TILES - 1:
                 read_page(k, 0, J)
             if k == PACK - 1:
+                nc.scalar.copy(
+                    x_bf16[0][:].rearrange("p (j t) -> p j t", t=PACK),
+                    x_flat[0][:].rearrange("p (t j) -> p j t", t=PACK),
+                )
                 quantize_x(0, 0, J)
             if 1 <= k <= PACK:
                 a, b = divmod(k - 1, PASSES)
-                w3q[a, b] = quantized_weight("w3_%d%d" % (a, b), w3, a, b, "stage%d" % (k - 1), b, "h%d" % (k + 1))
+                name = "w3_%d%d" % (a, b)
+                w3q[a, b] = quantized(name, rounded_weight(name, w3, a, b, k - 1, k - 1), "h%d" % (k + 1))
             if k == PACK:
                 w4_codes = tile("w4_codes", PASSES * N, U32)
                 nc.sync.dma_start(
@@ -321,11 +338,15 @@ def tile_list_tyre_slot_features_kernel(
                 )
                 if t == PACK - 1:
                     woven = z_bf16[b][:, PACK * c0 : PACK * c1]
-                    weave = nc.scalar.copy if (c, b) == (1, 0) else nc.vector.tensor_copy
-                    weave(
-                        woven.rearrange("p (c i t) -> p c t i", i=4, t=PACK),
-                        flat.rearrange("p (t c i) -> p c t i", i=4, t=PACK),
-                    )
+                    if (c, b) == (1, 0):
+                        nc.scalar.copy(
+                            woven.rearrange("p (j t) -> p j t", t=PACK), flat.rearrange("p (t j) -> p j t", t=PACK)
+                        )
+                    else:
+                        nc.vector.tensor_copy(
+                            woven.rearrange("p (c i t) -> p c t i", i=4, t=PACK),
+                            flat.rearrange("p (t c i) -> p c t i", i=4, t=PACK),
+                        )
                     nc.vector.quantize_mx(
                         out=z_codes[:, J * b + c0 : J * b + c1].bitcast(FP8X4),
                         scales=z_scales[:, J * b + c0 : J * b + c1],

@@ -1,6 +1,7 @@
 from contextlib import ExitStack
 
 import concourse.mybir as mybir
+from concourse.masks import make_identity
 
 K, T, S, H, T2, J, N = 1024, 2048, 512, 1024, 2048, 1024, 512
 FLOPS = 2 * (2 * K * H * S + H * H * J + H * N * J)
@@ -45,11 +46,11 @@ def tile_list_tyre_slot_features_kernel(
             nc.sync.dma_start(out=dst[:].bitcast(I32), in_=src.rearrange("p n i -> p (n i)").bitcast(I32))
             return dst
 
-        def load_scales_side_by_side(queue, dst, src):
-            for q in range(4):
-                queue.dma_start(
-                    out=dst[32 * q : 32 * q + 4, :].bitcast(I32).rearrange("r (a n) -> r a n", a=PASSES),
-                    in_=src[:, 4 * q : 4 * q + 4, :].rearrange("a r n -> r a n").bitcast(I32),
+        def load_scales_side_by_side(dst, src):
+            for r in range(4):
+                nc.sync.dma_start(
+                    out=dst[r:P:32, :].bitcast(I32).rearrange("q (a n) -> q a n", a=PASSES),
+                    in_=src[:, r:16:4, :].rearrange("a q n -> q a n").bitcast(I32),
                 )
 
         def load_scales_stacked(dst, src):
@@ -66,10 +67,29 @@ def tile_list_tyre_slot_features_kernel(
             )
             return dst
 
-        def load_gain(dst, src, t0, t1, quadrants=(0, 2, 1, 3)):
-            rows = src.rearrange("(q t) j -> q (t j)", t=PACK)
-            for q in quadrants:
-                nc.sync.dma_start(out=dst[32 * q : 32 * q + 32, t0 * S : t1 * S], in_=rows[:, t0 * S : t1 * S])
+        def load_gain(name, src):
+            rows = tile(name + "_rows", S, F32, "gain_rows")
+            nc.sync.dma_start(out=rows[:], in_=src)
+            return rows
+
+        def spread_gain(name, rows, banks):
+            turned = bank(name + "_turned", banks[0], S)
+            for u in range(S // P):
+                nc.tensor.transpose(turned[:, P * u : P * (u + 1)], rows[:, P * u : P * (u + 1)], identity[:])
+            spread = tile(name + "_spread", PACK * S, F32, "x_bf16_1")
+            for g in range(4):
+                nc.scalar.copy(
+                    spread[:].rearrange("j (t u g q) -> j g t u q", t=PACK, u=S // P, g=4)[:, g],
+                    turned[:].rearrange("j (u q t) -> j t u q", u=S // P, t=PACK),
+                )
+            gain = tile(name, PACK * S, F32)
+            for t in range(PACK):
+                back = bank(name + "_back%d" % t, banks[1 + t], S)
+                for u in range(S // P):
+                    cols = slice(S * t + P * u, S * t + P * (u + 1))
+                    nc.tensor.transpose(back[:, P * u : P * (u + 1)], spread[:, cols], identity[:])
+                nc.scalar.copy(gain[:, S * t : S * (t + 1)], back[:])
+            return gain
 
         page_rows = page0.rearrange("(b p t) n -> b t p n", b=PASSES, t=PACK)
         pages = {}
@@ -112,19 +132,21 @@ def tile_list_tyre_slot_features_kernel(
         idx2 = load_list("idx2", offs2)
         floor_sb = load_channel_vector("floor_sb", floor2)
         idx4 = load_list("idx4", offs4)
-        gain2 = tile("gain2", PACK * S, F32)
-        load_gain(gain2, wg2, 0, 1, (0,))
+        gain2_rows = load_gain("gain2", wg2)
         w2_raw = tile("w2_raw", PASSES * 2 * H, U8)
         nc.sync.dma_start(
             out=w2_raw[:].bitcast(I32).rearrange("p (a n) -> p a n", a=PASSES),
             in_=w2_words.rearrange("a p n -> p a n").bitcast(I32),
         )
         v2_table = [load_words("v2_table0", tab2_words[0], "stage0")]
-        load_gain(gain2, wg2, 0, 1, (2, 1))
-        load_scales_side_by_side(nc.sync, v2_table_scales, tab2_scales)
+        idx = load_list("idx", offs)
+        idx5 = load_list("idx5", offs5)
+        load_scales_side_by_side(v2_table_scales, tab2_scales)
         v2_table.append(load_words("v2_table1", tab2_words[1], "stage1"))
-        load_scales_side_by_side(nc.sync, w2_scales_raw, w2_scales)
-        load_gain(gain2, wg2, 0, 1, (3,))
+        load_scales_side_by_side(w2_scales_raw, w2_scales)
+        identity = tile("identity", P, F32)
+        make_identity(nc, identity[:])
+        gain2 = spread_gain("gain2", gain2_rows, (7, 6, 5, 4, 3))
 
         w2_codes = tile("w2_codes", PASSES * 2 * H, U8)
         for a in range(PASSES):
@@ -185,9 +207,8 @@ def tile_list_tyre_slot_features_kernel(
 
         put_h2(0)
         put_h2(1)
-        load_gain(gain2, wg2, 1, PACK)
+        gain1 = spread_gain("gain1", load_gain("gain1", wg1), (0, 1, 2, 0, 1))
         put_h2(2)
-        idx = load_list("idx", offs)
         load_scales_stacked(v_table_scales, tab_scales)
         v_scales = gather("v_scales", v_table_scales[:], idx, U8)
         v_codes = tile("v_codes", PASSES * S, U32)
@@ -236,11 +257,8 @@ def tile_list_tyre_slot_features_kernel(
         w1q[1, 1] = quantized("w1_11", rounded_weight("w1_11", w1, 1, 1, 3, 3), "h1")
         make_h1(1)
         idx3 = load_list("idx3", offs3)
-        idx5 = load_list("idx5", offs5)
         gx_sb = load_channel_vector("gx_sb", gx)
         gt_sb = load_channel_vector("gt_sb", gt)
-        gain1 = tile("gain1", PACK * S, F32)
-        load_gain(gain1, wg1, 0, PACK)
 
         w3q = {}
         x_bf16 = [tile("x_bf16_0", PACK * J, BF16, "gain2"), tile("x_bf16_1", PACK * J, BF16)]

from contextlib import ExitStack

import concourse.mybir as mybir
from concourse.masks import make_identity

K, T, S, H, T2, J, N = 1024, 2048, 512, 1024, 2048, 1024, 512
FLOPS = 2 * (2 * K * H * S + H * H * J + H * N * J)

F32, BF16 = mybir.dt.float32, mybir.dt.bfloat16
I32, U32, U16, U8 = mybir.dt.int32, mybir.dt.uint32, mybir.dt.uint16, mybir.dt.uint8
FP8X4, FP4X4 = mybir.dt.float8_e4m3fn_x4, mybir.dt.float4_e2m1fn_x4
ALU = mybir.AluOpType
ACT = mybir.ActivationFunctionType

P = 128
PACK = 4
KP = P * PACK
PASSES = 2
TILES = PASSES * PACK
CHUNKS = ((0, 256), (256, 768), (768, 1024))


def tile_list_tyre_slot_features_kernel(
    tc, tab_words, tab_scales, tab2_words, tab2_scales, offs, offs2, offs3, offs4, offs5, w1, g1,
    w2_words, w2_scales, floor2, page0, wg1, wg2, gx, w3, gt, w4_words, w4_scales, out,
):
    nc = tc.nc
    with ExitStack() as ctx:
        lists = ctx.enter_context(tc.tile_pool(name="lists", bufs=1))
        sb = ctx.enter_context(tc.tile_pool(name="sb", bufs=1))
        ps = ctx.enter_context(tc.psum_pool(name="ps", bufs=1))

        def tile(name, cols, dtype, slot=None):
            return sb.tile([P, cols], dtype, name=name, tag=slot or name, align_bytes=64)

        def bank(name, index, cols):
            return ps.tile([P, cols], F32, name=name, tag="bank%d" % index)

        def load_list(name, src):
            dst = lists.tile(list(src.shape), U16, name=name)
            nc.sync.dma_start(dst[:], src)
            return dst

        def load_words(name, src, slot):
            dst = tile(name, src.shape[1], U32, slot)
            nc.sync.dma_start(out=dst[:].bitcast(I32), in_=src.rearrange("p n i -> p (n i)").bitcast(I32))
            return dst

        def load_scales_side_by_side(dst, src):
            for r in range(4):
                nc.sync.dma_start(
                    out=dst[r:P:32, :].bitcast(I32).rearrange("q (a n) -> q a n", a=PASSES),
                    in_=src[:, r:16:4, :].rearrange("a q n -> q a n").bitcast(I32),
                )

        def load_scales_stacked(dst, src):
            for q in range(4):
                nc.sync.dma_start(
                    out=dst[32 * q : 32 * q + 8, :].bitcast(I32), in_=src[:, 4 * q : 4 * q + 4, :].bitcast(I32)
                )

        def load_channel_vector(name, src):
            dst = tile(name, TILES, F32)
            nc.sync.dma_start(
                out=dst[:].rearrange("p (b t) -> p b t", b=PASSES),
                in_=src.rearrange("(b p t) -> p b t", b=PASSES, t=PACK),
            )
            return dst

        def load_gain(name, src):
            rows = tile(name + "_rows", S, F32, "gain_rows")
            nc.sync.dma_start(out=rows[:], in_=src)
            return rows

        def spread_gain(name, rows, banks):
            turned = bank(name + "_turned", banks[0], S)
            for u in range(S // P):
                nc.tensor.transpose(turned[:, P * u : P * (u + 1)], rows[:, P * u : P * (u + 1)], identity[:])
            spread = tile(name + "_spread", PACK * S, F32, "x_bf16_1")
            for g in range(4):
                nc.scalar.copy(
                    spread[:].rearrange("j (t u g q) -> j g t u q", t=PACK, u=S // P, g=4)[:, g],
                    turned[:].rearrange("j (u q t) -> j t u q", u=S // P, t=PACK),
                )
            gain = tile(name, PACK * S, F32)
            for t in range(PACK):
                back = bank(name + "_back%d" % t, banks[1 + t], S)
                for u in range(S // P):
                    cols = slice(S * t + P * u, S * t + P * (u + 1))
                    nc.tensor.transpose(back[:, P * u : P * (u + 1)], spread[:, cols], identity[:])
                nc.scalar.copy(gain[:, S * t : S * (t + 1)], back[:])
            return gain

        page_rows = page0.rearrange("(b p t) n -> b t p n", b=PASSES, t=PACK)
        pages = {}

        def load_page(k):
            pages[k] = tile("page%d" % k, T2, F32)
            nc.sync.dma_start(out=pages[k][:], in_=page_rows[k // PACK, k % PACK])

        def gather(name, window, offsets, dtype):
            dst = tile(name, S, dtype)
            nc.vector.tensor_copy(dst[:], window.indirect(offsets[:]))
            return dst

        def rounded_weight(name, src, a, b, stage, turn):
            raw = tile(name + "_raw", PACK * KP, F32, "stage%d" % stage)
            nc.sync.dma_start(
                out=raw[:].rearrange("p (i c) -> p i c", i=PACK),
                in_=src[KP * a : KP * (a + 1), KP * b : KP * (b + 1)].rearrange("(p i) c -> p i c", i=PACK),
            )
            grouped = tile(name + "_bf16", PACK * KP, BF16, "grouped%d" % turn)
            dst = grouped[:].rearrange("p (t m i) -> p m t i", t=PACK, i=PACK)
            src_view = raw[:].rearrange("p (i m t) -> p m t i", i=PACK, t=PACK)
            for t in (0, 2):
                nc.scalar.copy(dst[:, :, t : t + 2, :], src_view[:, :, t : t + 2, :])
            return grouped

        def quantized(name, grouped, codes_slot=None):
            codes = tile(name + "_codes", KP, U32, codes_slot)
            scales = tile(name + "_scales", KP, U8)
            nc.vector.quantize_mx(out=codes[:].bitcast(FP8X4), scales=scales[:], in_=grouped[:])
            return codes, scales

        w2_scales_raw = tile("w2_scales_raw", PASSES * H, U8)
        v2_table_scales = tile("v2_table_scales", PASSES * T, U8)
        v_table_scales = tile("v_table_scales", T, U8)
        w4_planes = tile("w4_planes", N, U8)
        for plane in (v2_table_scales, w2_scales_raw, v_table_scales, w4_planes):
            nc.vector.memset(plane[:].bitcast(I32), 0)

        idx2 = load_list("idx2", offs2)
        floor_sb = load_channel_vector("floor_sb", floor2)
        idx4 = load_list("idx4", offs4)
        gain2_rows = load_gain("gain2", wg2)
        w2_raw = tile("w2_raw", PASSES * 2 * H, U8)
        nc.sync.dma_start(
            out=w2_raw[:].bitcast(I32).rearrange("p (a n) -> p a n", a=PASSES),
            in_=w2_words.rearrange("a p n -> p a n").bitcast(I32),
        )
        v2_table = [load_words("v2_table0", tab2_words[0], "stage0")]
        idx = load_list("idx", offs)
        idx5 = load_list("idx5", offs5)
        load_scales_side_by_side(v2_table_scales, tab2_scales)
        v2_table.append(load_words("v2_table1", tab2_words[1], "stage1"))
        load_scales_side_by_side(w2_scales_raw, w2_scales)
        identity = tile("identity", P, F32)
        make_identity(nc, identity[:])
        gain2 = spread_gain("gain2", gain2_rows, (7, 6, 5, 4, 3))

        w2_codes = tile("w2_codes", PASSES * 2 * H, U8)
        for a in range(PASSES):
            cols = slice(2 * H * a, 2 * H * (a + 1))
            nc.vector.tensor_copy(
                w2_codes[:, cols].rearrange("p (b t m e) -> p b t m e", b=PASSES, t=PACK, e=2),
                w2_raw[:, cols].rearrange("p (b m t e) -> p b t m e", b=PASSES, t=PACK, e=2),
            )

        def deal_w2_scales(b, slot):
            dealt = tile("w2_planes%d" % b, H, U8, slot)
            nc.vector.tensor_copy(
                dealt[:].rearrange("p (a t m) -> p a t m", a=PASSES, t=PACK),
                w2_scales_raw[:].rearrange("p (a b m t) -> p b a t m", a=PASSES, b=PASSES, t=PACK)[:, b],
            )
            return dealt

        v2_codes = [gather("v2_codes0", v2_table[0][:], idx2, U32)]
        v2_scales = [
            gather("v2_scales%d" % a, v2_table_scales[:, T * a : T * (a + 1)], idx2, U8) for a in range(PASSES)
        ]
        v2_codes.append(gather("v2_codes1", v2_table[1][:], idx2, U32))
        w2_planes = [deal_w2_scales(0, None), deal_w2_scales(1, "stage1")]

        order2 = [PACK * b + t for t in range(PACK) for b in range(PASSES)]
        h2_acc = {}
        for n, k in enumerate(order2):
            acc = h2_acc[k] = bank("h2_acc%d" % k, n, S)
            for a in range(PASSES):
                nc.tensor.matmul_mx(
                    out=acc[:],
                    lhsT=w2_codes[:, 2 * H * a + 2 * P * k : 2 * H * a + 2 * P * (k + 1)].bitcast(FP4X4),
                    lhsT_scale=w2_planes[k // PACK][:, KP * a + P * (k % PACK) : KP * a + P * (k % PACK + 1)],
                    rhs=v2_codes[a][:].bitcast(FP8X4),
                    rhs_scale=v2_scales[a][:],
                    start=(a == 0),
                    stop=(a == PASSES - 1),
                )

        def scatter(k, offsets, values, gain):
            t = k % PACK
            nc.vector.tensor_tensor(
                pages[k][:].indirect(offsets[:]), values[:], gain[:, S * t : S * (t + 1)], ALU.mult
            )

        h2_slots = ["h0", "v_scales", "v_codes", "h1", "w1_00_codes", "w1_10_codes", "grouped0", "grouped1"]

        def put_h2(n):
            k = order2[n]
            load_page(k)
            summed = h2_acc[k]
            if n > 0:
                summed = tile("h2_sum%d" % k, S, F32, "spill%d" % (n % 2))
                nc.scalar.copy(summed[:], h2_acc[k][:])
            h2 = tile("h2_%d" % k, S, F32, h2_slots[n])
            nc.vector.tensor_scalar(h2[:], summed[:], floor_sb[:, k : k + 1], None, ALU.max)
            scatter(k, idx4, h2, gain2)

        put_h2(0)
        put_h2(1)
        gain1 = spread_gain("gain1", load_gain("gain1", wg1), (0, 1, 2, 0, 1))
        put_h2(2)
        load_scales_stacked(v_table_scales, tab_scales)
        v_scales = gather("v_scales", v_table_scales[:], idx, U8)
        v_codes = tile("v_codes", PASSES * S, U32)
        for a in range(PASSES):
            table = load_words("v_table%d" % a, tab_words[a], "stage%d" % (2 + a))
            nc.vector.tensor_copy(v_codes[:, S * a : S * (a + 1)], table[:].indirect(idx[:]))
            if a == 0:
                put_h2(3)
        g1_sb = load_channel_vector("g1_sb", g1)
        w1q = {}
        for a in range(PASSES):
            rounded = rounded_weight("w1_%d0" % a, w1, a, 0, a, a)
            put_h2(4 + a)
            w1q[a, 0] = quantized("w1_%d0" % a, rounded)
        w1_01 = rounded_weight("w1_01", w1, 0, 1, 2, 2)
        put_h2(6)
        put_h2(7)

        h1 = {}

        def make_h1(b):
            for t in range(PACK):
                k = PACK * b + t
                acc = bank("h1_acc%d" % k, k, S)
                for a in range(PASSES):
                    codes, scales = w1q[a, b]
                    nc.tensor.matmul_mx(
                        out=acc[:],
                        lhsT=codes[:, P * t : P * (t + 1)].bitcast(FP8X4),
                        lhsT_scale=scales[:, P * t : P * (t + 1)],
                        rhs=v_codes[:, S * a : S * (a + 1)].bitcast(FP8X4),
                        rhs_scale=v_scales[4 * a :, :],
                        start=(a == 0),
                        stop=(a == PASSES - 1),
                    )
                gate = tile("gate%d" % k, S, F32, "grouped3" if k == PACK - 1 else "spill%d" % (k % 2))
                nc.scalar.activation(gate[:], acc[:], ACT.Sigmoid)
                if k == TILES - 1:
                    h1[k] = gate
                else:
                    h1[k] = tile("h1_%d" % k, S, F32, "h%d" % k)
                    nc.scalar.activation(h1[k][:], gate[:], ACT.Copy, scale=g1_sb[:, k : k + 1])

        make_h1(0)
        w1q[0, 1] = quantized("w1_01", w1_01, "h0")
        w1q[1, 1] = quantized("w1_11", rounded_weight("w1_11", w1, 1, 1, 3, 3), "h1")
        make_h1(1)
        idx3 = load_list("idx3", offs3)
        gx_sb = load_channel_vector("gx_sb", gx)
        gt_sb = load_channel_vector("gt_sb", gt)

        w3q = {}
        x_bf16 = [tile("x_bf16_0", PACK * J, BF16, "gain2"), tile("x_bf16_1", PACK * J, BF16)]
        x_codes = [tile("x_codes0", J, U32, "w2_raw"), tile("x_codes1", J, U32, "v2_table_scales")]
        x_scales = [tile("x_scales%d" % a, J, U8) for a in range(PASSES)]
        seen = {}
        x_flat = []

        def read_page(k, c0, c1):
            a, t = divmod(k, PACK)
            nc.vector.tensor_copy(seen[k][:, c0:c1], pages[k][:].indirect(idx5[:, c0 // 16 : c1 // 16]))
            if k == 0:
                x_flat.append(tile("x_flat", PACK * J, BF16, "page0"))
            if a == 0:
                dst = x_flat[0][:, J * t : J * (t + 1)]
            else:
                dst = x_bf16[a][:, PACK * c0 + t : PACK * c1 : PACK]
            nc.scalar.activation(dst, seen[k][:, c0:c1], ACT.Copy, scale=gx_sb[:, k : k + 1])

        def quantize_x(a, c0, c1):
            nc.vector.quantize_mx(
                out=x_codes[a][:, c0:c1].bitcast(FP8X4),
                scales=x_scales[a][:, c0:c1],
                in_=x_bf16[a][:, PACK * c0 : PACK * c1],
            )

        for k in range(TILES):
            if k == TILES - 1:
                gate = h1[k]
                h1[k] = tile("h1_%d" % k, S, F32, "gain2")
                nc.vector.tensor_scalar(h1[k][:], gate[:], g1_sb[:, k : k + 1], None, ALU.mult)
            scatter(k, idx3, h1[k], gain1)
            seen[k] = tile("seen%d" % k, J, F32)
            if k < TILES - 1:
                read_page(k, 0, J)
            if k == PACK - 1:
                nc.scalar.copy(
                    x_bf16[0][:].rearrange("p (j t) -> p j t", t=PACK),
                    x_flat[0][:].rearrange("p (t j) -> p j t", t=PACK),
                )
                quantize_x(0, 0, J)
            if 1 <= k <= PACK:
                a, b = divmod(k - 1, PASSES)
                name = "w3_%d%d" % (a, b)
                w3q[a, b] = quantized(name, rounded_weight(name, w3, a, b, k - 1, k - 1), "h%d" % (k + 1))
            if k == PACK:
                w4_codes = tile("w4_codes", PASSES * N, U32)
                nc.sync.dma_start(
                    out=w4_codes[:].bitcast(I32).rearrange("p (a n) -> p a n", a=PASSES),
                    in_=w4_words.rearrange("a p n i -> p a (n i)").bitcast(I32),
                )
                load_scales_stacked(w4_planes, w4_scales)
        for c0, c1 in CHUNKS:
            read_page(TILES - 1, c0, c1)
        for c0, c1 in CHUNKS:
            quantize_x(1, c0, c1)

        def product3(acc, k, a, c0, c1):
            b, t = divmod(k, PACK)
            codes, scales = w3q[a, b]
            nc.tensor.matmul_mx(
                out=acc[:],
                lhsT=codes[:, P * t : P * (t + 1)].bitcast(FP8X4),
                lhsT_scale=scales[:, P * t : P * (t + 1)],
                rhs=x_codes[a][:, c0:c1].bitcast(FP8X4),
                rhs_scale=x_scales[a][:, c0:c1],
                start=(a == 0),
                stop=(a == PASSES - 1),
            )

        y_ring = [tile("y_ring%d" % i, PACK * 512, F32, "stage%d" % i) for i in range(PASSES)]
        z_flat = [tile("z_flat%d" % b, PACK * J, BF16, "stage%d" % (2 + b)) for b in range(PASSES)]
        z_bf16 = [tile("z_bf16_%d" % b, PACK * J, BF16, "page%d" % (4 * b)) for b in range(PASSES)]
        z_codes = tile("z_codes", PASSES * J, U32, "page1")
        z_scales = tile("z_scales", PASSES * J, U8, "v_table_scales")
        staged = [tile("staged%d" % i, PACK * 512, F32, "page%d" % (2 + i)) for i in range(2)]

        def make_z(c, c0, c1):
            width = c1 - c0
            accs = [bank("y_acc%d_%d" % (c, k), k, width) for k in range(TILES)] if c == 0 else {}
            if c == 0:
                for k in range(TILES):
                    product3(accs[k], k, 0, c0, c1)
            for k in range(TILES):
                b, t = divmod(k, PACK)
                if c > 0:
                    accs[k] = bank("y_acc%d_%d" % (c, k), k if c == 1 else k % 4, width)
                    product3(accs[k], k, 0, c0, c1)
                product3(accs[k], k, 1, c0, c1)
                y = y_ring[b][:, 512 * t : 512 * t + width]
                nc.scalar.activation(y, accs[k][:], ACT.Tanh)
                flat = z_flat[b][:, PACK * c0 : PACK * c1]
                nc.vector.scalar_tensor_tensor(
                    flat[:, width * t : width * (t + 1)], y, gt_sb[:, k : k + 1], seen[k][:, c0:c1], ALU.mult, ALU.add
                )
                if t == PACK - 1:
                    woven = z_bf16[b][:, PACK * c0 : PACK * c1]
                    if (c, b) == (1, 0):
                        nc.scalar.copy(
                            woven.rearrange("p (j t) -> p j t", t=PACK), flat.rearrange("p (t j) -> p j t", t=PACK)
                        )
                    else:
                        nc.vector.tensor_copy(
                            woven.rearrange("p (c i t) -> p c t i", i=4, t=PACK),
                            flat.rearrange("p (t c i) -> p c t i", i=4, t=PACK),
                        )
                    nc.vector.quantize_mx(
                        out=z_codes[:, J * b + c0 : J * b + c1].bitcast(FP8X4),
                        scales=z_scales[:, J * b + c0 : J * b + c1],
                        in_=woven,
                    )

        def make_out(c, c0, c1):
            width = c1 - c0
            accs = [bank("out_acc%d_%d" % (c, n), 4 + n, width) for n in range(N // P)]
            for a in range(PASSES):
                for n in range(N // P):
                    nc.tensor.matmul_mx(
                        out=accs[n][:],
                        lhsT=w4_codes[:, N * a + P * n : N * a + P * (n + 1)].bitcast(FP8X4),
                        lhsT_scale=w4_planes[4 * a :, P * n : P * (n + 1)],
                        rhs=z_codes[:, J * a + c0 : J * a + c1].bitcast(FP8X4),
                        rhs_scale=z_scales[:, J * a + c0 : J * a + c1],
                        start=(a == 0),
                        stop=(a == PASSES - 1),
                    )
            last = c == len(CHUNKS) - 1
            for n in range(N // P):
                result = staged[c % 2][:, 512 * n : 512 * n + width]
                if last and n % 2 == 1:
                    nc.vector.tensor_copy(result, accs[n][:])
                else:
                    nc.scalar.copy(result, accs[n][:])
                nc.sync.dma_start(out=out[P * n : P * (n + 1), c0:c1], in_=result)

        for c, (c0, c1) in enumerate(CHUNKS):
            make_z(c, c0, c1)
            if c > 0:
                make_out(c - 1, *CHUNKS[c - 1])
        make_out(len(CHUNKS) - 1, *CHUNKS[-1])
